import numpy as np
import ml_dtypes


def mxq(x, axis, fmt="e4m3"):
    dtype, down = {"e4m3": (ml_dtypes.float8_e4m3fn, 7), "e5m2": (ml_dtypes.float8_e5m2, 14)}[fmt]
    v = np.moveaxis(np.asarray(x, np.float32).astype(ml_dtypes.bfloat16).astype(np.float64), axis, -1)
    blocks = v.reshape(v.shape[:-1] + (-1, 32))
    amax = np.abs(blocks).max(-1, keepdims=True)
    byte = np.maximum(np.where(amax > 0, np.frexp(amax)[1] - 1 + 127, 0) - down, 1)
    scale = np.exp2(byte - 127.0)
    codes = (blocks / scale).astype(np.float32).astype(dtype).astype(np.float64)
    return np.moveaxis((codes * scale).reshape(v.shape), -1, axis)


WIDE = False


def mx_kscale(k):
    if not WIDE:
        return np.ones(k)
    levels = np.array([30, -30])
    if k % 512:
        return np.exp2(np.random.permutation(np.resize(levels, k // 32))).repeat(32)
    a = np.empty((k // 512, 16))
    for p in range(k // 512):
        a[p, :8] = np.random.permutation(np.resize(levels, 8))
        for g in range(8):
            far = levels[np.abs(levels - a[p, g]) >= 10]
            a[p, g + 8] = far[np.random.randint(len(far))]
    return np.exp2(a.ravel()).repeat(32)


BF16 = ml_dtypes.bfloat16


def bf(x):
    return np.asarray(x, np.float32).astype(BF16)


def f64(x):
    return np.asarray(x).astype(np.float64)


E2M1 = np.array([0.0, 0.5, 1.0, 1.5, 2.0, 3.0, 4.0, 6.0, -0.0, -0.5, -1.0, -1.5, -2.0, -3.0, -4.0, -6.0])


def pack_weight(w, fmt):
    k, n = w.shape
    w = f64(bf(w)).reshape(k // 32, 32, n)
    amax = np.abs(w).max(1)
    if fmt in ("e4m3", "e5m2"):
        byte = np.frexp(amax)[1] - 1 + 127 - (7 if fmt == "e4m3" else 14)
    else:
        mant, ex = np.frexp(amax / 6.0)
        byte = np.where(mant > 0.5, ex, ex - 1) + 127
    byte = np.clip(np.where(amax > 0, byte, 1), 1, 254)
    scaled = (w * np.exp2(127.0 - byte)[:, None, :]).reshape(k, n).astype(np.float32)
    by_word = np.ascontiguousarray(scaled.reshape(k // 512, 128, 4, n).transpose(0, 1, 3, 2))
    if fmt in ("e4m3", "e5m2"):
        words = by_word.astype(ml_dtypes.float8_e4m3fn if fmt == "e4m3" else ml_dtypes.float8_e5m2).view(np.uint8)
    else:
        c = by_word.astype(ml_dtypes.float4_e2m1fn).view(np.uint8) & 0xF
        words = c[..., 0::2] | (c[..., 1::2] << 4)
    return np.ascontiguousarray(words), np.ascontiguousarray(byte.astype(np.uint8).reshape(k // 512, 16, n))


def unpack_weight(words, scales, fmt):
    g, p, n, _ = words.shape
    if fmt in ("e4m3", "e5m2"):
        vals = np.ascontiguousarray(words).view(ml_dtypes.float8_e4m3fn if fmt == "e4m3" else ml_dtypes.float8_e5m2).astype(np.float64)
    else:
        nib = np.empty((g, p, n, 4), np.uint8)
        nib[..., 0::2] = words & 0xF
        nib[..., 1::2] = words >> 4
        vals = E2M1[nib]
    vals = vals * np.repeat(np.exp2(scales.astype(np.float64) - 127.0), 8, axis=1)[..., None]
    return vals.transpose(0, 1, 3, 2).reshape(g * 512, n)


C, B, O, I = 6, 256, 1024, 512


def setup_inputs():
    s = mx_kscale(O)
    G = np.random.standard_t(5, (O, C * 2 * B)) * s[:, None]
    g_words, g_scales = pack_weight(G, "e5m2")
    return {"g_words": g_words,
            "g_scales": g_scales,
            "w_re": bf(np.random.standard_normal((C, I, O)) / np.sqrt(2 * O) / s),
            "w_im": bf(np.random.standard_normal((C, I, O)) / np.sqrt(2 * O) / s),
            "gain": bf(1 + 0.1 * np.random.standard_normal((C, I)))}


def reference(g_words, g_scales, w_re, w_im, gain):
    G = unpack_weight(g_words, g_scales, "e5m2")
    dy = G.reshape(O, C, 2 * B).transpose(1, 2, 0)
    wr = mxq(f64(w_re), 2, "e4m3").swapaxes(1, 2)
    wi = mxq(f64(w_im), 2, "e4m3").swapaxes(1, 2)
    u = dy @ wr
    v = dy @ wi
    d = f64(gain)[:, None, :]
    dx_re = (u[:, :B] + v[:, B:]) * d
    dx_im = (u[:, B:] - v[:, :B]) * d
    return dx_re, dx_im

@@ -1,0 +1,170 @@
+from contextlib import ExitStack
+
+import concourse.mybir as mybir
+from concourse.masks import make_identity
+
+C, B, O, I = 6, 256, 1024, 512
+FLOPS = 2 * 2 * C * (2 * B) * O * I
+
+F32 = mybir.dt.float32
+BF16 = mybir.dt.bfloat16
+I32 = mybir.dt.int32
+U32 = mybir.dt.uint32
+U8 = mybir.dt.uint8
+E4M3 = mybir.dt.float8_e4m3fn_x4
+E5M2 = mybir.dt.float8_e5m2_x4
+MULT = mybir.AluOpType.mult
+SUB = mybir.AluOpType.subtract
+
+P = 128
+G = 2
+N = 2 * B
+STEPS = 2 * C
+SHUFFLE_FROM = 99
+
+
+def tile_fourier_mode_input_gradient_e1_kernel(tc, g_words, g_scales, w_re, w_im, gain, out_0, out_1):
+    nc = tc.nc
+    with ExitStack() as ctx:
+        keep = ctx.enter_context(tc.tile_pool(name="keep", bufs=1))
+        wpool = ctx.enter_context(tc.tile_pool(name="wpool", bufs=16))
+        work = ctx.enter_context(tc.tile_pool(name="work", bufs=4))
+        qpool = ctx.enter_context(tc.tile_pool(name="qpool", bufs=8))
+        tpsum = ctx.enter_context(tc.psum_pool(name="tpsum", bufs=4))
+        apsum = ctx.enter_context(tc.psum_pool(name="apsum", bufs=4))
+        ctx.enter_context(tc.manual_schedule())
+
+        ident = keep.tile([P, P], F32, name="ident")
+        make_identity(nc, ident[:])
+
+        gs_first = keep.tile([P, G, N], U8, name="gs_first", align_bytes=64)
+        gs_rest = keep.tile([P, G, (C - 1) * N], U8, name="gs_rest", align_bytes=64)
+        nc.vector.memset(gs_first[:].rearrange("p g n -> p (g n)").bitcast(I32), 0)
+        nc.vector.memset(gs_rest[:].rearrange("p g n -> p (g n)").bitcast(I32), 0)
+
+        def load_scales(queue, plane, cols):
+            for quad in range(4):
+                queue.dma_start(
+                    out=plane[32 * quad : 32 * quad + 4, :, :].bitcast(I32),
+                    in_=g_scales[:, 4 * quad : 4 * quad + 4, cols].rearrange("g r n -> r g n").bitcast(I32),
+                )
+
+        gain_rows = keep.tile([P, C // 2, 8], BF16, name="gain_rows")
+        nc.scalar.dma_start(out=gain_rows[:], in_=gain.rearrange("c i -> (c i)").rearrange("(s p j) -> p s j", p=P, j=8))
+        load_scales(nc.scalar, gs_first, slice(0, N))
+
+        raw = {}
+        g_codes = {}
+        g_bytes = g_words.rearrange("g p n t -> p g (n t)")
+        for c in range(C):
+            for part, w in enumerate((w_re, w_im)):
+                for h in range(2):
+                    chunk = wpool.tile([P, 2 * O], BF16, name="chunk")
+                    nc.sync.dma_start(out=chunk[:], in_=w[c, 256 * h : 256 * (h + 1), :].rearrange("(p q) o -> p (q o)", q=2))
+                    raw[2 * c + part, h] = chunk
+            g_codes[c] = keep.tile([P, G, N], U32, name="g_codes%d" % c, align_bytes=64)
+            nc.sync.dma_start(out=g_codes[c][:].bitcast(I32), in_=g_bytes[:, :, 4 * N * c : 4 * N * (c + 1)].bitcast(I32))
+            if c == 1:
+                load_scales(nc.sync, gs_rest, slice(N, C * N))
+
+        gain_all = keep.tile([P, C * I], BF16, name="gain_all")
+        gain_words = gain_rows[:].rearrange("p s j -> p (s j)").bitcast(F32)
+        for s in range(C // 2):
+            bank = tpsum.tile([P, 4, P], F32, name="bank")
+            for j in range(4):
+                nc.tensor.transpose(bank[:, j, :], gain_words[:, 4 * s + j : 4 * s + j + 1].to_broadcast([P, P]), ident[:])
+            nc.scalar.copy(
+                out=gain_all[:].bitcast(F32)[:, 512 * s : 512 * (s + 1)].rearrange("p (n j) -> p n j", j=4),
+                in_=bank[:].rearrange("p j n -> p n j"),
+            )
+
+        shuffled = {}
+        grouped = {}
+        codes = {}
+        scales = {}
+        results = {}
+
+        def shuffle(s, h):
+            if s < SHUFFLE_FROM or s >= STEPS:
+                return
+            split = work.tile([P, 4, 2, P], F32, name="split", bufs=5)
+            nc.vector.tensor_copy(out=split[:], in_=raw[s, h][:].bitcast(F32).rearrange("p (a m u) -> p a u m", a=4, u=2))
+            shuffled[s, h] = split
+
+        def transposes(s):
+            for g in range(G):
+                grouped[s, g] = work.tile([P, 4 * I], BF16, name="grouped", align_bytes=64)
+            order = [(g, h) for h in range(2) for g in range(G)] if s < 2 else [(g, h) for g in range(G) for h in range(2)]
+            for g, h in order:
+                bank = tpsum.tile([P, 4, P], F32, name="bank")
+                for q in range(2):
+                    for u in range(2):
+                        if (s, h) in shuffled:
+                            src = shuffled[s, h][:, 2 * q + g, u, :]
+                        else:
+                            first = 512 * q + 256 * g
+                            src = raw[s, h][:].bitcast(F32)[:, first + u : first + 256 : 2]
+                        nc.tensor.transpose(bank[:, 2 * q + u, :], src, ident[:])
+                nc.scalar.copy(
+                    out=grouped[s, g][:].bitcast(F32)[:, 512 * h : 512 * (h + 1)].rearrange("k (p j) -> k p j", j=4),
+                    in_=bank[:].rearrange("k j p -> k p j"),
+                )
+            for g in range(G):
+                codes[s, g] = qpool.tile([P, I], U32, name="codes", align_bytes=64)
+                scales[s, g] = qpool.tile([P, I], U8, name="scales", align_bytes=64)
+                nc.vector.quantize_mx(out=codes[s, g][:].bitcast(E4M3), scales=scales[s, g][:], in_=grouped[s, g][:])
+
+        def product(c, terms):
+            acc = apsum.tile([P, I], F32, name="acc")
+            passes = [(col, s, g) for col, s in terms for g in range(G)]
+            for n, (col, s, g) in enumerate(passes):
+                plane = gs_first[:, g, col : col + P] if c == 0 else gs_rest[:, g, (c - 1) * N + col : (c - 1) * N + col + P]
+                nc.tensor.matmul_mx(
+                    out=acc[:],
+                    lhsT=g_codes[c][:, g, col : col + P].bitcast(E5M2),
+                    lhsT_scale=plane,
+                    rhs=codes[s, g][:].bitcast(E4M3),
+                    rhs_scale=scales[s, g][:],
+                    start=(n == 0),
+                    stop=(n == len(passes) - 1),
+                )
+            return acc
+
+        def multiply(k, shuffle_step):
+            c, t = divmod(k, 2)
+            re_col, im_col = P * t, B + P * t
+            wr, wi = 2 * c, 2 * c + 1
+            gain_c = gain_all[:, I * c : I * (c + 1)]
+            re_wi = product(c, [(re_col, wi)])
+            subtrahend = work.tile([P, I], F32, name="subtrahend", bufs=2)
+            nc.scalar.copy(out=subtrahend[:], in_=re_wi[:])
+            im_wr = product(c, [(im_col, wr)])
+            real = product(c, [(re_col, wr), (im_col, wi)])
+            diff = work.tile([P, I], F32, name="diff", bufs=2)
+            res_re = keep.tile([P, I], F32, name="res_re%d" % k)
+            res_im = keep.tile([P, I], F32, name="res_im%d" % k)
+            nc.vector.tensor_tensor(out=diff[:], in0=im_wr[:], in1=subtrahend[:], op=SUB)
+            shuffle(shuffle_step, 0)
+            nc.vector.tensor_tensor(out=res_re[:], in0=real[:], in1=gain_c, op=MULT)
+            nc.vector.tensor_tensor(out=res_im[:], in0=diff[:], in1=gain_c, op=MULT)
+            shuffle(shuffle_step, 1)
+            results[k] = (res_re, res_im)
+
+        transposes(0)
+        transposes(1)
+        multiply(0, 3)
+        transposes(2)
+        multiply(1, 4)
+        transposes(3)
+        transposes(4)
+        shuffle(5, 0)
+        shuffle(5, 1)
+        for k in range(2, STEPS):
+            multiply(k, k + 4)
+            if k + 3 < STEPS:
+                transposes(k + 3)
+
+        for k in range(STEPS):
+            c, t = divmod(k, 2)
+            nc.sync.dma_start(out=out_0[c, P * t : P * (t + 1), :], in_=results[k][0][:])
+            nc.sync.dma_start(out=out_1[c, P * t : P * (t + 1), :], in_=results[k][1][:])

@@ -17,154 +17,201 @@ MULT = mybir.AluOpType.mult
 SUB = mybir.AluOpType.subtract
 
 P = 128
-G = 2
+PASSES = 2
 N = 2 * B
-STEPS = 2 * C
-SHUFFLE_FROM = 99
+RE, IM = 0, 1
 
 
 def tile_fourier_mode_input_gradient_e1_kernel(tc, g_words, g_scales, w_re, w_im, gain, out_0, out_1):
     nc = tc.nc
     with ExitStack() as ctx:
         keep = ctx.enter_context(tc.tile_pool(name="keep", bufs=1))
-        wpool = ctx.enter_context(tc.tile_pool(name="wpool", bufs=16))
+        wpool = ctx.enter_context(tc.tile_pool(name="wpool", bufs=8))
         work = ctx.enter_context(tc.tile_pool(name="work", bufs=4))
-        qpool = ctx.enter_context(tc.tile_pool(name="qpool", bufs=8))
+        qpool = ctx.enter_context(tc.tile_pool(name="qpool", bufs=6))
         tpsum = ctx.enter_context(tc.psum_pool(name="tpsum", bufs=4))
-        apsum = ctx.enter_context(tc.psum_pool(name="apsum", bufs=4))
+        apsum = ctx.enter_context(tc.psum_pool(name="apsum", bufs=2))
         ctx.enter_context(tc.manual_schedule())
 
         ident = keep.tile([P, P], F32, name="ident")
         make_identity(nc, ident[:])
 
-        gs_first = keep.tile([P, G, N], U8, name="gs_first", align_bytes=64)
-        gs_rest = keep.tile([P, G, (C - 1) * N], U8, name="gs_rest", align_bytes=64)
-        nc.vector.memset(gs_first[:].rearrange("p g n -> p (g n)").bitcast(I32), 0)
-        nc.vector.memset(gs_rest[:].rearrange("p g n -> p (g n)").bitcast(I32), 0)
+        g_planes = keep.tile([P, C // 2, PASSES, 2 * N], U8, name="g_planes", align_bytes=64)
+        for pair in range(C // 2):
+            nc.vector.memset(g_planes[:, pair].rearrange("p g n -> p (g n)").bitcast(I32), 0)
 
-        def load_scales(queue, plane, cols):
-            for quad in range(4):
+        def load_scales(queue, pair):
+            for r in range(4):
                 queue.dma_start(
-                    out=plane[32 * quad : 32 * quad + 4, :, :].bitcast(I32),
-                    in_=g_scales[:, 4 * quad : 4 * quad + 4, cols].rearrange("g r n -> r g n").bitcast(I32),
+                    out=g_planes[r:P:32, pair].bitcast(I32),
+                    in_=g_scales[:, r:16:4, 2 * N * pair : 2 * N * (pair + 1)].rearrange("g q n -> q g n").bitcast(I32),
                 )
 
-        gain_rows = keep.tile([P, C // 2, 8], BF16, name="gain_rows")
-        nc.scalar.dma_start(out=gain_rows[:], in_=gain.rearrange("c i -> (c i)").rearrange("(s p j) -> p s j", p=P, j=8))
-        load_scales(nc.scalar, gs_first, slice(0, N))
-
         raw = {}
-        g_codes = {}
+        g_codes = keep.tile([P, C, PASSES, N], U32, name="g_codes", align_bytes=64)
         g_bytes = g_words.rearrange("g p n t -> p g (n t)")
-        for c in range(C):
-            for part, w in enumerate((w_re, w_im)):
-                for h in range(2):
-                    chunk = wpool.tile([P, 2 * O], BF16, name="chunk")
-                    nc.sync.dma_start(out=chunk[:], in_=w[c, 256 * h : 256 * (h + 1), :].rearrange("(p q) o -> p (q o)", q=2))
-                    raw[2 * c + part, h] = chunk
-            g_codes[c] = keep.tile([P, G, N], U32, name="g_codes%d" % c, align_bytes=64)
-            nc.sync.dma_start(out=g_codes[c][:].bitcast(I32), in_=g_bytes[:, :, 4 * N * c : 4 * N * (c + 1)].bitcast(I32))
-            if c == 1:
-                load_scales(nc.sync, gs_rest, slice(N, C * N))
+
+        def load_weight(c, part):
+            raw[c, part] = wpool.tile([P, 4 * O], BF16, name="raw")
+            rows = (w_re, w_im)[part][c].rearrange("(p q) o -> p (q o)", q=4)
+            pieces = 2 if c == 0 else 1
+            width = 4 * O // pieces
+            for n in range(pieces):
+                nc.sync.dma_start(out=raw[c, part][:, width * n : width * (n + 1)], in_=rows[:, width * n : width * (n + 1)])
+
+        def load_g(c):
+            nc.sync.dma_start(out=g_codes[:, c].bitcast(I32), in_=g_bytes[:, :, 4 * N * c : 4 * N * (c + 1)].bitcast(I32))
+
+        gain_rows = keep.tile([P, C // 2, 8], BF16, name="gain_rows")
+        load_weight(0, RE)
+        nc.scalar.dma_start(out=gain_rows[:], in_=gain.rearrange("c i -> (c i)").rearrange("(s p j) -> p s j", p=P, j=8))
+        load_scales(nc.scalar, 0)
+        load_g(0)
+        load_weight(0, IM)
+        for c in range(1, C):
+            load_weight(c, RE)
+            load_weight(c, IM)
+            if c % 2 == 0:
+                load_scales(nc.sync, c // 2)
+            load_g(c)
+
+        split = {}
+        grouped = {}
+        codes = {}
+        scales = {}
+        real = {}
+        minuend = {}
+        diff = {}
+        results = {}
+
+        def split_words(copy, c, part, g, rows=slice(0, 4)):
+            if (c, part, g) not in split:
+                split[c, part, g] = work.tile([P, 4, 2, P], F32, name="split")
+            words = raw[c, part][:].bitcast(F32).rearrange("p (q g m u) -> p g q u m", q=4, g=PASSES, u=2)
+            copy(out=split[c, part, g][:, rows], in_=words[:, g, rows])
+
+        def transposes(c, part):
+            for g in range(PASSES):
+                grouped[c, part, g] = work.tile([P, 4 * I], BF16, name="grouped", align_bytes=64)
+            first = (c, part) == (0, RE)
+            order = [(g, j) for j in range(2) for g in range(PASSES)] if first else [(g, j) for g in range(PASSES) for j in range(2)]
+            for g, j in order:
+                bank = tpsum.tile([P, 4, P], F32, name="bank")
+                for q in (2 * j, 2 * j + 1):
+                    for u in range(2):
+                        nc.tensor.transpose(bank[:, 2 * (q % 2) + u, :], split[c, part, g][:, q, u, :], ident[:])
+                nc.scalar.copy(
+                    out=grouped[c, part, g][:].bitcast(F32).rearrange("k (p j w) -> k j p w", j=2, w=4)[:, j],
+                    in_=bank[:].rearrange("k w p -> k p w"),
+                )
+
+        def quantise(c, part, g):
+            codes[c, part, g] = qpool.tile([P, I], U32, name="codes", align_bytes=64)
+            scales[c, part, g] = qpool.tile([P, I], U8, name="scales", align_bytes=64)
+            nc.vector.quantize_mx(out=codes[c, part, g][:].bitcast(E4M3), scales=scales[c, part, g][:], in_=grouped[c, part, g][:])
+
+        def product(acc, c, g_part, t, w_part, start, stop):
+            col = B * g_part + P * t
+            for g in range(PASSES):
+                plane_col = N * (c % 2) + col
+                nc.tensor.matmul_mx(
+                    out=acc[:],
+                    lhsT=g_codes[:, c, g, col : col + P].bitcast(E5M2),
+                    lhsT_scale=g_planes[:, c // 2, g, plane_col : plane_col + P],
+                    rhs=codes[c, w_part, g][:].bitcast(E4M3),
+                    rhs_scale=scales[c, w_part, g][:],
+                    start=start and g == 0,
+                    stop=stop and g == PASSES - 1,
+                )
+
+        def products_with_w_re(c):
+            for t in range(2):
+                cross = apsum.tile([P, I], F32, name="cross")
+                product(cross, c, IM, t, RE, True, True)
+                minuend[t] = work.tile([P, I], F32, name="minuend", bufs=2)
+                nc.scalar.copy(out=minuend[t][:], in_=cross[:])
+            for t in range(2):
+                real[t] = apsum.tile([P, I], F32, name="real")
+                product(real[t], c, RE, t, RE, True, False)
+
+        def products_with_w_im(c):
+            subtrahend = {}
+            for t in range(2):
+                subtrahend[t] = apsum.tile([P, I], F32, name="cross")
+                product(subtrahend[t], c, RE, t, IM, True, True)
+                product(real[t], c, IM, t, IM, False, True)
+            return subtrahend
+
+        def subtract(t, subtrahend):
+            diff[t] = work.tile([P, I], F32, name="diff", bufs=2)
+            nc.vector.tensor_tensor(out=diff[t][:], in0=minuend[t][:], in1=subtrahend[:], op=SUB)
+
+        def apply_gain(c, part, t):
+            results[c, part, t] = keep.tile([P, I], F32, name="result_%d_%d_%d" % (c, part, t))
+            nc.vector.tensor_tensor(out=results[c, part, t][:], in0=(real, diff)[part][t][:], in1=gain_all[:, I * c : I * (c + 1)], op=MULT)
+
+        gain_wide = keep.tile([P, 2 * C, P], F32, name="gain_wide")
+        gain_words = gain_rows[:].rearrange("p s j -> p (s j)").bitcast(F32)
+        for j in range(2):
+            for g in range(PASSES):
+                split_words(nc.vector.tensor_copy, 0, RE, g, slice(2 * j, 2 * j + 2))
+        nc.vector.tensor_copy(out=gain_wide[:], in_=gain_words.unsqueeze(2).to_broadcast([P, 2 * C, P]))
+        transposes(0, RE)
 
         gain_all = keep.tile([P, C * I], BF16, name="gain_all")
-        gain_words = gain_rows[:].rearrange("p s j -> p (s j)").bitcast(F32)
         for s in range(C // 2):
             bank = tpsum.tile([P, 4, P], F32, name="bank")
             for j in range(4):
-                nc.tensor.transpose(bank[:, j, :], gain_words[:, 4 * s + j : 4 * s + j + 1].to_broadcast([P, P]), ident[:])
+                nc.tensor.transpose(bank[:, j, :], gain_wide[:, 4 * s + j, :], ident[:])
             nc.scalar.copy(
                 out=gain_all[:].bitcast(F32)[:, 512 * s : 512 * (s + 1)].rearrange("p (n j) -> p n j", j=4),
                 in_=bank[:].rearrange("p j n -> p n j"),
             )
 
-        shuffled = {}
-        grouped = {}
-        codes = {}
-        scales = {}
-        results = {}
+        quantise(0, RE, 0)
+        quantise(0, RE, 1)
+        products_with_w_re(0)
+        split_words(nc.vector.tensor_copy, 0, IM, 0)
+        split_words(nc.vector.tensor_copy, 0, IM, 1)
+        transposes(0, IM)
+        split_words(nc.vector.tensor_copy, 1, RE, 0)
+        split_words(nc.vector.tensor_copy, 1, RE, 1)
+        quantise(0, IM, 0)
+        quantise(0, IM, 1)
+        transposes(1, RE)
 
-        def shuffle(s, h):
-            if s < SHUFFLE_FROM or s >= STEPS:
-                return
-            split = work.tile([P, 4, 2, P], F32, name="split", bufs=5)
-            nc.vector.tensor_copy(out=split[:], in_=raw[s, h][:].bitcast(F32).rearrange("p (a m u) -> p a u m", a=4, u=2))
-            shuffled[s, h] = split
+        for c in range(C):
+            more = c + 1 < C
+            most = c + 2 < C
+            if more:
+                quantise(c + 1, RE, 0)
+            subtrahend = products_with_w_im(c)
+            subtract(0, subtrahend[0])
+            if more:
+                split_words(nc.vector.tensor_copy, c + 1, IM, 0)
+                split_words(nc.scalar.copy, c + 1, IM, 1)
+            apply_gain(c, RE, 0)
+            if more:
+                quantise(c + 1, RE, 1)
+            subtract(1, subtrahend[1])
+            apply_gain(c, RE, 1)
+            if more:
+                transposes(c + 1, IM)
+            if most:
+                split_words(nc.vector.tensor_copy, c + 2, RE, 0)
+            if more:
+                quantise(c + 1, IM, 0)
+                products_with_w_re(c + 1)
+            if most:
+                split_words(nc.vector.tensor_copy, c + 2, RE, 1)
+            apply_gain(c, IM, 0)
+            if more:
+                quantise(c + 1, IM, 1)
+            apply_gain(c, IM, 1)
+            if most:
+                transposes(c + 2, RE)
 
-        def transposes(s):
-            for g in range(G):
-                grouped[s, g] = work.tile([P, 4 * I], BF16, name="grouped", align_bytes=64)
-            order = [(g, h) for h in range(2) for g in range(G)] if s < 2 else [(g, h) for g in range(G) for h in range(2)]
-            for g, h in order:
-                bank = tpsum.tile([P, 4, P], F32, name="bank")
-                for q in range(2):
-                    for u in range(2):
-                        if (s, h) in shuffled:
-                            src = shuffled[s, h][:, 2 * q + g, u, :]
-                        else:
-                            first = 512 * q + 256 * g
-                            src = raw[s, h][:].bitcast(F32)[:, first + u : first + 256 : 2]
-                        nc.tensor.transpose(bank[:, 2 * q + u, :], src, ident[:])
-                nc.scalar.copy(
-                    out=grouped[s, g][:].bitcast(F32)[:, 512 * h : 512 * (h + 1)].rearrange("k (p j) -> k p j", j=4),
-                    in_=bank[:].rearrange("k j p -> k p j"),
-                )
-            for g in range(G):
-                codes[s, g] = qpool.tile([P, I], U32, name="codes", align_bytes=64)
-                scales[s, g] = qpool.tile([P, I], U8, name="scales", align_bytes=64)
-                nc.vector.quantize_mx(out=codes[s, g][:].bitcast(E4M3), scales=scales[s, g][:], in_=grouped[s, g][:])
-
-        def product(c, terms):
-            acc = apsum.tile([P, I], F32, name="acc")
-            passes = [(col, s, g) for col, s in terms for g in range(G)]
-            for n, (col, s, g) in enumerate(passes):
-                plane = gs_first[:, g, col : col + P] if c == 0 else gs_rest[:, g, (c - 1) * N + col : (c - 1) * N + col + P]
-                nc.tensor.matmul_mx(
-                    out=acc[:],
-                    lhsT=g_codes[c][:, g, col : col + P].bitcast(E5M2),
-                    lhsT_scale=plane,
-                    rhs=codes[s, g][:].bitcast(E4M3),
-                    rhs_scale=scales[s, g][:],
-                    start=(n == 0),
-                    stop=(n == len(passes) - 1),
-                )
-            return acc
-
-        def multiply(k, shuffle_step):
-            c, t = divmod(k, 2)
-            re_col, im_col = P * t, B + P * t
-            wr, wi = 2 * c, 2 * c + 1
-            gain_c = gain_all[:, I * c : I * (c + 1)]
-            re_wi = product(c, [(re_col, wi)])
-            subtrahend = work.tile([P, I], F32, name="subtrahend", bufs=2)
-            nc.scalar.copy(out=subtrahend[:], in_=re_wi[:])
-            im_wr = product(c, [(im_col, wr)])
-            real = product(c, [(re_col, wr), (im_col, wi)])
-            diff = work.tile([P, I], F32, name="diff", bufs=2)
-            res_re = keep.tile([P, I], F32, name="res_re%d" % k)
-            res_im = keep.tile([P, I], F32, name="res_im%d" % k)
-            nc.vector.tensor_tensor(out=diff[:], in0=im_wr[:], in1=subtrahend[:], op=SUB)
-            shuffle(shuffle_step, 0)
-            nc.vector.tensor_tensor(out=res_re[:], in0=real[:], in1=gain_c, op=MULT)
-            nc.vector.tensor_tensor(out=res_im[:], in0=diff[:], in1=gain_c, op=MULT)
-            shuffle(shuffle_step, 1)
-            results[k] = (res_re, res_im)
-
-        transposes(0)
-        transposes(1)
-        multiply(0, 3)
-        transposes(2)
-        multiply(1, 4)
-        transposes(3)
-        transposes(4)
-        shuffle(5, 0)
-        shuffle(5, 1)
-        for k in range(2, STEPS):
-            multiply(k, k + 4)
-            if k + 3 < STEPS:
-                transposes(k + 3)
-
-        for k in range(STEPS):
-            c, t = divmod(k, 2)
-            nc.sync.dma_start(out=out_0[c, P * t : P * (t + 1), :], in_=results[k][0][:])
-            nc.sync.dma_start(out=out_1[c, P * t : P * (t + 1), :], in_=results[k][1][:])
+        for c in range(C):
+            for part in (RE, IM):
+                for t in range(2):
+                    nc.sync.dma_start(out=(out_0, out_1)[part][c, P * t : P * (t + 1), :], in_=results[c, part, t][:])

@@ -76,6 +76,7 @@ def tile_fourier_mode_input_gradient_e1_kernel(tc, g_words, g_scales, w_re, w_im
             load_g(c)
 
         split = {}
+        is_split = set()
         grouped = {}
         codes = {}
         scales = {}
@@ -84,11 +85,12 @@ def tile_fourier_mode_input_gradient_e1_kernel(tc, g_words, g_scales, w_re, w_im
         diff = {}
         results = {}
 
-        def split_words(copy, c, part, g, rows=slice(0, 4)):
-            if (c, part, g) not in split:
-                split[c, part, g] = work.tile([P, 4, 2, P], F32, name="split")
-            words = raw[c, part][:].bitcast(F32).rearrange("p (q g m u) -> p g q u m", q=4, g=PASSES, u=2)
-            copy(out=split[c, part, g][:, rows], in_=words[:, g, rows])
+        def split_words(copy, c, part, passes, rows=slice(0, 4)):
+            if (c, part) not in split:
+                split[c, part] = work.tile([P, 4, PASSES, 2, P], F32, name="split", bufs=2)
+            words = raw[c, part][:].bitcast(F32).rearrange("p (q g m u) -> p q g u m", q=4, g=PASSES, u=2)
+            copy(out=split[c, part][:, rows, passes], in_=words[:, rows, passes])
+            is_split.update((c, part, g) for g in range(passes.start, passes.stop))
 
         def transposes(c, part):
             for g in range(PASSES):
@@ -99,7 +101,12 @@ def tile_fourier_mode_input_gradient_e1_kernel(tc, g_words, g_scales, w_re, w_im
                 bank = tpsum.tile([P, 4, P], F32, name="bank")
                 for q in (2 * j, 2 * j + 1):
                     for u in range(2):
-                        nc.tensor.transpose(bank[:, 2 * (q % 2) + u, :], split[c, part, g][:, q, u, :], ident[:])
+                        if (c, part, g) in is_split:
+                            src = split[c, part][:, q, g, u, :]
+                        else:
+                            start = 512 * q + 256 * g
+                            src = raw[c, part][:].bitcast(F32)[:, start + u : start + 256 : 2]
+                        nc.tensor.transpose(bank[:, 2 * (q % 2) + u, :], src, ident[:])
                 nc.scalar.copy(
                     out=grouped[c, part, g][:].bitcast(F32).rearrange("k (p j w) -> k j p w", j=2, w=4)[:, j],
                     in_=bank[:].rearrange("k w p -> k p w"),
@@ -110,51 +117,54 @@ def tile_fourier_mode_input_gradient_e1_kernel(tc, g_words, g_scales, w_re, w_im
             scales[c, part, g] = qpool.tile([P, I], U8, name="scales", align_bytes=64)
             nc.vector.quantize_mx(out=codes[c, part, g][:].bitcast(E4M3), scales=scales[c, part, g][:], in_=grouped[c, part, g][:])
 
-        def product(acc, c, g_part, t, w_part, start, stop):
+        def one_pass(acc, c, g_part, t, w_part, g, start, stop):
             col = B * g_part + P * t
-            for g in range(PASSES):
-                plane_col = N * (c % 2) + col
-                nc.tensor.matmul_mx(
-                    out=acc[:],
-                    lhsT=g_codes[:, c, g, col : col + P].bitcast(E5M2),
-                    lhsT_scale=g_planes[:, c // 2, g, plane_col : plane_col + P],
-                    rhs=codes[c, w_part, g][:].bitcast(E4M3),
-                    rhs_scale=scales[c, w_part, g][:],
-                    start=start and g == 0,
-                    stop=stop and g == PASSES - 1,
-                )
+            plane_col = N * (c % 2) + col
+            nc.tensor.matmul_mx(
+                out=acc[:],
+                lhsT=g_codes[:, c, g, col : col + P].bitcast(E5M2),
+                lhsT_scale=g_planes[:, c // 2, g, plane_col : plane_col + P],
+                rhs=codes[c, w_part, g][:].bitcast(E4M3),
+                rhs_scale=scales[c, w_part, g][:],
+                start=start,
+                stop=stop,
+            )
 
         def products_with_w_re(c):
+            cross = [apsum.tile([P, I], F32, name="cross") for t in range(2)]
+            for g in range(PASSES):
+                for t in range(2):
+                    one_pass(cross[t], c, IM, t, RE, g, g == 0, g == PASSES - 1)
             for t in range(2):
-                cross = apsum.tile([P, I], F32, name="cross")
-                product(cross, c, IM, t, RE, True, True)
                 minuend[t] = work.tile([P, I], F32, name="minuend", bufs=2)
-                nc.scalar.copy(out=minuend[t][:], in_=cross[:])
+                nc.scalar.copy(out=minuend[t][:], in_=cross[t][:])
             for t in range(2):
                 real[t] = apsum.tile([P, I], F32, name="real")
-                product(real[t], c, RE, t, RE, True, False)
+                for g in range(PASSES):
+                    one_pass(real[t], c, RE, t, RE, g, g == 0, False)
 
         def products_with_w_im(c):
-            subtrahend = {}
+            cross = [apsum.tile([P, I], F32, name="cross") for t in range(2)]
             for t in range(2):
-                subtrahend[t] = apsum.tile([P, I], F32, name="cross")
-                product(subtrahend[t], c, RE, t, IM, True, True)
-                product(real[t], c, IM, t, IM, False, True)
-            return subtrahend
+                for g in range(PASSES):
+                    one_pass(cross[t], c, RE, t, IM, g, g == 0, g == PASSES - 1)
+                for g in range(PASSES):
+                    one_pass(real[t], c, IM, t, IM, g, False, g == PASSES - 1)
+            return cross
 
         def subtract(t, subtrahend):
             diff[t] = work.tile([P, I], F32, name="diff", bufs=2)
             nc.vector.tensor_tensor(out=diff[t][:], in0=minuend[t][:], in1=subtrahend[:], op=SUB)
 
-        def apply_gain(c, part, t):
+        def apply_gain(engine, c, part, t):
             results[c, part, t] = keep.tile([P, I], F32, name="result_%d_%d_%d" % (c, part, t))
-            nc.vector.tensor_tensor(out=results[c, part, t][:], in0=(real, diff)[part][t][:], in1=gain_all[:, I * c : I * (c + 1)], op=MULT)
+            engine.tensor_tensor(out=results[c, part, t][:], in0=(real, diff)[part][t][:], in1=gain_all[:, I * c : I * (c + 1)], op=MULT)
 
         gain_wide = keep.tile([P, 2 * C, P], F32, name="gain_wide")
         gain_words = gain_rows[:].rearrange("p s j -> p (s j)").bitcast(F32)
         for j in range(2):
             for g in range(PASSES):
-                split_words(nc.vector.tensor_copy, 0, RE, g, slice(2 * j, 2 * j + 2))
+                split_words(nc.vector.tensor_copy, 0, RE, slice(g, g + 1), slice(2 * j, 2 * j + 2))
         nc.vector.tensor_copy(out=gain_wide[:], in_=gain_words.unsqueeze(2).to_broadcast([P, 2 * C, P]))
         transposes(0, RE)
 
@@ -171,14 +181,16 @@ def tile_fourier_mode_input_gradient_e1_kernel(tc, g_words, g_scales, w_re, w_im
         quantise(0, RE, 0)
         quantise(0, RE, 1)
         products_with_w_re(0)
-        split_words(nc.vector.tensor_copy, 0, IM, 0)
-        split_words(nc.vector.tensor_copy, 0, IM, 1)
+        split_words(nc.vector.tensor_copy, 0, IM, slice(0, 1))
+        split_words(nc.vector.tensor_copy, 0, IM, slice(1, 2))
         transposes(0, IM)
-        split_words(nc.vector.tensor_copy, 1, RE, 0)
-        split_words(nc.vector.tensor_copy, 1, RE, 1)
+        split_words(nc.vector.tensor_copy, 1, RE, slice(0, 1))
+        split_words(nc.vector.tensor_copy, 1, RE, slice(1, 2))
         quantise(0, IM, 0)
         quantise(0, IM, 1)
         transposes(1, RE)
+
+        split_words(nc.vector.tensor_copy, 1, IM, slice(0, 1))
 
         for c in range(C):
             more = c + 1 < C
@@ -187,31 +199,24 @@ def tile_fourier_mode_input_gradient_e1_kernel(tc, g_words, g_scales, w_re, w_im
                 quantise(c + 1, RE, 0)
             subtrahend = products_with_w_im(c)
             subtract(0, subtrahend[0])
-            if more:
-                split_words(nc.vector.tensor_copy, c + 1, IM, 0)
-                split_words(nc.scalar.copy, c + 1, IM, 1)
-            apply_gain(c, RE, 0)
+            apply_gain(nc.gpsimd, c, IM, 0)
+            apply_gain(nc.vector, c, RE, 0)
+            subtract(1, subtrahend[1])
+            apply_gain(nc.vector, c, RE, 1)
             if more:
                 quantise(c + 1, RE, 1)
-            subtract(1, subtrahend[1])
-            apply_gain(c, RE, 1)
-            if more:
                 transposes(c + 1, IM)
-            if most:
-                split_words(nc.vector.tensor_copy, c + 2, RE, 0)
-            if more:
-                quantise(c + 1, IM, 0)
                 products_with_w_re(c + 1)
             if most:
-                split_words(nc.vector.tensor_copy, c + 2, RE, 1)
-            apply_gain(c, IM, 0)
+                split_words(nc.vector.tensor_copy, c + 2, RE, slice(0, 2))
             if more:
+                quantise(c + 1, IM, 0)
                 quantise(c + 1, IM, 1)
-            apply_gain(c, IM, 1)
             if most:
                 transposes(c + 2, RE)
+                split_words(nc.vector.tensor_copy, c + 2, IM, slice(0, 1))
+            apply_gain(nc.vector, c, IM, 1)
 
         for c in range(C):
-            for part in (RE, IM):
-                for t in range(2):
-                    nc.sync.dma_start(out=(out_0, out_1)[part][c, P * t : P * (t + 1), :], in_=results[c, part, t][:])
+            for part, t in ((RE, 0), (IM, 0), (RE, 1), (IM, 1)):
+                nc.sync.dma_start(out=(out_0, out_1)[part][c, P * t : P * (t + 1), :], in_=results[c, part, t][:])

@@ -17,13 +17,19 @@ MULT = mybir.AluOpType.mult
 SUB = mybir.AluOpType.subtract
 
 P = 128
-PASSES = 2
-N = 2 * B
+PASSES = O // (4 * P)
+G_COLS = 2 * B
+ROWS = I // P
+TILES = B // P
+GROUPS = C // 2
 RE, IM = 0, 1
+EARLY_STORES = 2
 
 
 def tile_fourier_mode_input_gradient_e1_kernel(tc, g_words, g_scales, w_re, w_im, gain, out_0, out_1):
     nc = tc.nc
+    weights = (w_re, w_im)
+    outs = (out_0, out_1)
     with ExitStack() as ctx:
         keep = ctx.enter_context(tc.tile_pool(name="keep", bufs=1))
         wpool = ctx.enter_context(tc.tile_pool(name="wpool", bufs=8))
@@ -36,33 +42,37 @@ def tile_fourier_mode_input_gradient_e1_kernel(tc, g_words, g_scales, w_re, w_im
         ident = keep.tile([P, P], F32, name="ident")
         make_identity(nc, ident[:])
 
-        g_planes = keep.tile([P, C // 2, PASSES, 2 * N], U8, name="g_planes", align_bytes=64)
-        for pair in range(C // 2):
-            nc.vector.memset(g_planes[:, pair].rearrange("p g n -> p (g n)").bitcast(I32), 0)
+        g_planes = keep.tile([P, GROUPS, PASSES, 2 * G_COLS], U8, name="g_planes", align_bytes=64)
+        for group in range(GROUPS):
+            nc.vector.memset(g_planes[:, group].rearrange("p g n -> p (g n)").bitcast(I32), 0)
 
-        def load_scales(queue, pair):
+        def load_scales(queue, group):
+            cols = slice(2 * G_COLS * group, 2 * G_COLS * (group + 1))
             for r in range(4):
                 queue.dma_start(
-                    out=g_planes[r:P:32, pair].bitcast(I32),
-                    in_=g_scales[:, r:16:4, 2 * N * pair : 2 * N * (pair + 1)].rearrange("g q n -> q g n").bitcast(I32),
+                    out=g_planes[r:P:32, group].bitcast(I32),
+                    in_=g_scales[:, r:16:4, cols].rearrange("g q n -> q g n").bitcast(I32),
                 )
 
         raw = {}
-        g_codes = keep.tile([P, C, PASSES, N], U32, name="g_codes", align_bytes=64)
-        g_bytes = g_words.rearrange("g p n t -> p g (n t)")
+        g_codes = keep.tile([P, C, PASSES, G_COLS], U32, name="g_codes", align_bytes=64)
+        g_bytes = g_words.rearrange("g k n e -> k g (n e)")
 
         def load_weight(c, part):
-            raw[c, part] = wpool.tile([P, 4 * O], BF16, name="raw")
-            rows = (w_re, w_im)[part][c].rearrange("(p q) o -> p (q o)", q=4)
+            raw[c, part] = wpool.tile([P, ROWS * O], BF16, name="raw")
+            rows = weights[part][c].rearrange("(p q) o -> p (q o)", q=ROWS)
             pieces = 2 if c == 0 else 1
-            width = 4 * O // pieces
+            width = ROWS * O // pieces
             for n in range(pieces):
                 nc.sync.dma_start(out=raw[c, part][:, width * n : width * (n + 1)], in_=rows[:, width * n : width * (n + 1)])
 
         def load_g(c):
-            nc.sync.dma_start(out=g_codes[:, c].bitcast(I32), in_=g_bytes[:, :, 4 * N * c : 4 * N * (c + 1)].bitcast(I32))
+            nc.sync.dma_start(
+                out=g_codes[:, c].bitcast(I32),
+                in_=g_bytes[:, :, 4 * G_COLS * c : 4 * G_COLS * (c + 1)].bitcast(I32),
+            )
 
-        gain_rows = keep.tile([P, C // 2, 8], BF16, name="gain_rows")
+        gain_rows = keep.tile([P, GROUPS, 8], BF16, name="gain_rows")
         load_weight(0, RE)
         nc.scalar.dma_start(out=gain_rows[:], in_=gain.rearrange("c i -> (c i)").rearrange("(s p j) -> p s j", p=P, j=8))
         load_scales(nc.scalar, 0)
@@ -76,7 +86,6 @@ def tile_fourier_mode_input_gradient_e1_kernel(tc, g_words, g_scales, w_re, w_im
             load_g(c)
 
         split = {}
-        is_split = set()
         grouped = {}
         codes = {}
         scales = {}
@@ -85,31 +94,26 @@ def tile_fourier_mode_input_gradient_e1_kernel(tc, g_words, g_scales, w_re, w_im
         diff = {}
         results = {}
 
-        def split_words(copy, c, part, passes, rows=slice(0, 4)):
+        def split_pairs(copy, c, part, passes, rows=slice(0, ROWS)):
             if (c, part) not in split:
-                split[c, part] = work.tile([P, 4, PASSES, 2, P], F32, name="split", bufs=2)
-            words = raw[c, part][:].bitcast(F32).rearrange("p (q g m u) -> p q g u m", q=4, g=PASSES, u=2)
-            copy(out=split[c, part][:, rows, passes], in_=words[:, rows, passes])
-            is_split.update((c, part, g) for g in range(passes.start, passes.stop))
+                split[c, part] = work.tile([P, ROWS, PASSES, 2, P], F32, name="split", bufs=2)
+            pairs = raw[c, part][:].bitcast(F32).rearrange("p (q g k u) -> p q g u k", q=ROWS, g=PASSES, u=2)
+            copy(out=split[c, part][:, rows, passes], in_=pairs[:, rows, passes])
 
         def transposes(c, part):
             for g in range(PASSES):
                 grouped[c, part, g] = work.tile([P, 4 * I], BF16, name="grouped", align_bytes=64)
-            first = (c, part) == (0, RE)
-            order = [(g, j) for j in range(2) for g in range(PASSES)] if first else [(g, j) for g in range(PASSES) for j in range(2)]
+            if (c, part) == (0, RE):
+                order = [(g, j) for j in range(2) for g in range(PASSES)]
+            else:
+                order = [(g, j) for g in range(PASSES) for j in range(2)]
             for g, j in order:
                 bank = tpsum.tile([P, 4, P], F32, name="bank")
-                for q in (2 * j, 2 * j + 1):
-                    for u in range(2):
-                        if (c, part, g) in is_split:
-                            src = split[c, part][:, q, g, u, :]
-                        else:
-                            start = 512 * q + 256 * g
-                            src = raw[c, part][:].bitcast(F32)[:, start + u : start + 256 : 2]
-                        nc.tensor.transpose(bank[:, 2 * (q % 2) + u, :], src, ident[:])
+                for slot in range(4):
+                    nc.tensor.transpose(bank[:, slot, :], split[c, part][:, 2 * j + slot // 2, g, slot % 2, :], ident[:])
                 nc.scalar.copy(
-                    out=grouped[c, part, g][:].bitcast(F32).rearrange("k (p j w) -> k j p w", j=2, w=4)[:, j],
-                    in_=bank[:].rearrange("k w p -> k p w"),
+                    out=grouped[c, part, g][:].bitcast(F32).rearrange("k (p j slot) -> k j p slot", j=2, slot=4)[:, j],
+                    in_=bank[:].rearrange("k slot p -> k p slot"),
                 )
 
         def quantise(c, part, g):
@@ -117,9 +121,9 @@ def tile_fourier_mode_input_gradient_e1_kernel(tc, g_words, g_scales, w_re, w_im
             scales[c, part, g] = qpool.tile([P, I], U8, name="scales", align_bytes=64)
             nc.vector.quantize_mx(out=codes[c, part, g][:].bitcast(E4M3), scales=scales[c, part, g][:], in_=grouped[c, part, g][:])
 
-        def one_pass(acc, c, g_part, t, w_part, g, start, stop):
-            col = B * g_part + P * t
-            plane_col = N * (c % 2) + col
+        def one_pass(acc, c, dy_part, t, w_part, g, start, stop):
+            col = B * dy_part + P * t
+            plane_col = G_COLS * (c % 2) + col
             nc.tensor.matmul_mx(
                 out=acc[:],
                 lhsT=g_codes[:, c, g, col : col + P].bitcast(E5M2),
@@ -131,21 +135,21 @@ def tile_fourier_mode_input_gradient_e1_kernel(tc, g_words, g_scales, w_re, w_im
             )
 
         def products_with_w_re(c):
-            cross = [apsum.tile([P, I], F32, name="cross") for t in range(2)]
+            cross = [apsum.tile([P, I], F32, name="cross") for t in range(TILES)]
             for g in range(PASSES):
-                for t in range(2):
+                for t in range(TILES):
                     one_pass(cross[t], c, IM, t, RE, g, g == 0, g == PASSES - 1)
-            for t in range(2):
-                minuend[t] = work.tile([P, I], F32, name="minuend", bufs=2)
+            for t in range(TILES):
+                minuend[t] = work.tile([P, I], F32, name="minuend", bufs=TILES)
                 nc.scalar.copy(out=minuend[t][:], in_=cross[t][:])
-            for t in range(2):
+            for t in range(TILES):
                 real[t] = apsum.tile([P, I], F32, name="real")
                 for g in range(PASSES):
                     one_pass(real[t], c, RE, t, RE, g, g == 0, False)
 
         def products_with_w_im(c):
-            cross = [apsum.tile([P, I], F32, name="cross") for t in range(2)]
-            for t in range(2):
+            cross = [apsum.tile([P, I], F32, name="cross") for t in range(TILES)]
+            for t in range(TILES):
                 for g in range(PASSES):
                     one_pass(cross[t], c, RE, t, IM, g, g == 0, g == PASSES - 1)
                 for g in range(PASSES):
@@ -153,49 +157,56 @@ def tile_fourier_mode_input_gradient_e1_kernel(tc, g_words, g_scales, w_re, w_im
             return cross
 
         def subtract(t, subtrahend):
-            diff[t] = work.tile([P, I], F32, name="diff", bufs=2)
+            diff[t] = work.tile([P, I], F32, name="diff", bufs=TILES)
             nc.vector.tensor_tensor(out=diff[t][:], in0=minuend[t][:], in1=subtrahend[:], op=SUB)
 
         def apply_gain(engine, c, part, t):
-            results[c, part, t] = keep.tile([P, I], F32, name="result_%d_%d_%d" % (c, part, t))
-            engine.tensor_tensor(out=results[c, part, t][:], in0=(real, diff)[part][t][:], in1=gain_all[:, I * c : I * (c + 1)], op=MULT)
+            if (c, part) not in results:
+                results[c, part] = keep.tile([P, TILES, I], F32, name="result_%d_%d" % (c, part))
+            engine.tensor_tensor(out=results[c, part][:, t], in0=(real, diff)[part][t][:], in1=gain_all[:, I * c : I * (c + 1)], op=MULT)
 
-        gain_wide = keep.tile([P, 2 * C, P], F32, name="gain_wide")
-        gain_words = gain_rows[:].rearrange("p s j -> p (s j)").bitcast(F32)
+        both_passes = slice(0, PASSES)
+        first_pass, second_pass = slice(0, 1), slice(1, 2)
+
+        gain_wide = keep.tile([P, 4 * GROUPS, P], F32, name="gain_wide")
+        gain_pairs = gain_rows[:].rearrange("p s j -> p (s j)").bitcast(F32)
         for j in range(2):
-            for g in range(PASSES):
-                split_words(nc.vector.tensor_copy, 0, RE, slice(g, g + 1), slice(2 * j, 2 * j + 2))
-        nc.vector.tensor_copy(out=gain_wide[:], in_=gain_words.unsqueeze(2).to_broadcast([P, 2 * C, P]))
+            for passes in (first_pass, second_pass):
+                split_pairs(nc.vector.tensor_copy, 0, RE, passes, slice(2 * j, 2 * j + 2))
+        nc.vector.tensor_copy(out=gain_wide[:], in_=gain_pairs.unsqueeze(2).to_broadcast([P, 4 * GROUPS, P]))
         transposes(0, RE)
 
         gain_all = keep.tile([P, C * I], BF16, name="gain_all")
-        for s in range(C // 2):
+        for group in range(GROUPS):
             bank = tpsum.tile([P, 4, P], F32, name="bank")
-            for j in range(4):
-                nc.tensor.transpose(bank[:, j, :], gain_wide[:, 4 * s + j, :], ident[:])
+            for slot in range(4):
+                nc.tensor.transpose(bank[:, slot, :], gain_wide[:, 4 * group + slot, :], ident[:])
             nc.scalar.copy(
-                out=gain_all[:].bitcast(F32)[:, 512 * s : 512 * (s + 1)].rearrange("p (n j) -> p n j", j=4),
-                in_=bank[:].rearrange("p j n -> p n j"),
+                out=gain_all[:].bitcast(F32)[:, I * group : I * (group + 1)].rearrange("m (p slot) -> m p slot", slot=4),
+                in_=bank[:].rearrange("m slot p -> m p slot"),
             )
 
         quantise(0, RE, 0)
         quantise(0, RE, 1)
         products_with_w_re(0)
-        split_words(nc.vector.tensor_copy, 0, IM, slice(0, 1))
-        split_words(nc.vector.tensor_copy, 0, IM, slice(1, 2))
+        split_pairs(nc.vector.tensor_copy, 0, IM, first_pass)
+        split_pairs(nc.vector.tensor_copy, 0, IM, second_pass)
         transposes(0, IM)
-        split_words(nc.vector.tensor_copy, 1, RE, slice(0, 1))
-        split_words(nc.vector.tensor_copy, 1, RE, slice(1, 2))
+        split_pairs(nc.vector.tensor_copy, 1, RE, first_pass)
+        split_pairs(nc.vector.tensor_copy, 1, RE, second_pass)
         quantise(0, IM, 0)
         quantise(0, IM, 1)
         transposes(1, RE)
-
-        split_words(nc.vector.tensor_copy, 1, IM, slice(0, 1))
+        split_pairs(nc.vector.tensor_copy, 1, IM, first_pass)
 
         for c in range(C):
-            more = c + 1 < C
-            most = c + 2 < C
-            if more:
+            has_next = c + 1 < C
+            has_second_next = c + 2 < C
+            if 0 < c <= EARLY_STORES:
+                for part in (RE, IM):
+                    nc.gpsimd.dma_start(out=outs[part][c - 1].rearrange("(t p) i -> p t i", p=P), in_=results[c - 1, part][:])
+            if has_next:
+                split_pairs(nc.scalar.copy, c + 1, IM, second_pass)
                 quantise(c + 1, RE, 0)
             subtrahend = products_with_w_im(c)
             subtract(0, subtrahend[0])
@@ -203,20 +214,21 @@ def tile_fourier_mode_input_gradient_e1_kernel(tc, g_words, g_scales, w_re, w_im
             apply_gain(nc.vector, c, RE, 0)
             subtract(1, subtrahend[1])
             apply_gain(nc.vector, c, RE, 1)
-            if more:
+            if has_next:
                 quantise(c + 1, RE, 1)
                 transposes(c + 1, IM)
                 products_with_w_re(c + 1)
-            if most:
-                split_words(nc.vector.tensor_copy, c + 2, RE, slice(0, 2))
-            if more:
+            if has_second_next:
+                split_pairs(nc.vector.tensor_copy, c + 2, RE, both_passes)
+            if has_next:
                 quantise(c + 1, IM, 0)
                 quantise(c + 1, IM, 1)
-            if most:
+            if has_second_next:
                 transposes(c + 2, RE)
-                split_words(nc.vector.tensor_copy, c + 2, IM, slice(0, 1))
+                split_pairs(nc.vector.tensor_copy, c + 2, IM, first_pass)
             apply_gain(nc.vector, c, IM, 1)
 
-        for c in range(C):
-            for part, t in ((RE, 0), (IM, 0), (RE, 1), (IM, 1)):
-                nc.sync.dma_start(out=(out_0, out_1)[part][c, P * t : P * (t + 1), :], in_=results[c, part, t][:])
+        for c in range(EARLY_STORES, C):
+            for t in range(TILES):
+                for part in (RE, IM):
+                    nc.sync.dma_start(out=outs[part][c, P * t : P * (t + 1), :], in_=results[c, part][:, t])

from contextlib import ExitStack

import concourse.mybir as mybir
from concourse.masks import make_identity

C, B, O, I = 6, 256, 1024, 512
FLOPS = 2 * 2 * C * (2 * B) * O * I

F32 = mybir.dt.float32
BF16 = mybir.dt.bfloat16
I32 = mybir.dt.int32
U32 = mybir.dt.uint32
U8 = mybir.dt.uint8
E4M3 = mybir.dt.float8_e4m3fn_x4
E5M2 = mybir.dt.float8_e5m2_x4
MULT = mybir.AluOpType.mult
SUB = mybir.AluOpType.subtract

P = 128
PASSES = O // (4 * P)
G_COLS = 2 * B
ROWS = I // P
TILES = B // P
GROUPS = C // 2
RE, IM = 0, 1
EARLY_STORES = 2


def tile_fourier_mode_input_gradient_e1_kernel(tc, g_words, g_scales, w_re, w_im, gain, out_0, out_1):
    nc = tc.nc
    weights = (w_re, w_im)
    outs = (out_0, out_1)
    with ExitStack() as ctx:
        keep = ctx.enter_context(tc.tile_pool(name="keep", bufs=1))
        wpool = ctx.enter_context(tc.tile_pool(name="wpool", bufs=8))
        work = ctx.enter_context(tc.tile_pool(name="work", bufs=4))
        qpool = ctx.enter_context(tc.tile_pool(name="qpool", bufs=6))
        tpsum = ctx.enter_context(tc.psum_pool(name="tpsum", bufs=4))
        apsum = ctx.enter_context(tc.psum_pool(name="apsum", bufs=2))
        ctx.enter_context(tc.manual_schedule())

        ident = keep.tile([P, P], F32, name="ident")
        make_identity(nc, ident[:])

        g_planes = keep.tile([P, GROUPS, PASSES, 2 * G_COLS], U8, name="g_planes", align_bytes=64)
        for group in range(GROUPS):
            nc.vector.memset(g_planes[:, group].rearrange("p g n -> p (g n)").bitcast(I32), 0)

        def load_scales(queue, group):
            cols = slice(2 * G_COLS * group, 2 * G_COLS * (group + 1))
            for r in range(4):
                queue.dma_start(
                    out=g_planes[r:P:32, group].bitcast(I32),
                    in_=g_scales[:, r:16:4, cols].rearrange("g q n -> q g n").bitcast(I32),
                )

        raw = {}
        g_codes = keep.tile([P, C, PASSES, G_COLS], U32, name="g_codes", align_bytes=64)
        g_bytes = g_words.rearrange("g k n e -> k g (n e)")

        def load_weight(c, part):
            raw[c, part] = wpool.tile([P, ROWS * O], BF16, name="raw")
            rows = weights[part][c].rearrange("(p q) o -> p (q o)", q=ROWS)
            pieces = 2 if c == 0 else 1
            width = ROWS * O // pieces
            for n in range(pieces):
                nc.sync.dma_start(out=raw[c, part][:, width * n : width * (n + 1)], in_=rows[:, width * n : width * (n + 1)])

        def load_g(c):
            nc.sync.dma_start(
                out=g_codes[:, c].bitcast(I32),
                in_=g_bytes[:, :, 4 * G_COLS * c : 4 * G_COLS * (c + 1)].bitcast(I32),
            )

        gain_rows = keep.tile([P, GROUPS, 8], BF16, name="gain_rows")
        load_weight(0, RE)
        nc.scalar.dma_start(out=gain_rows[:], in_=gain.rearrange("c i -> (c i)").rearrange("(s p j) -> p s j", p=P, j=8))
        load_scales(nc.scalar, 0)
        load_g(0)
        load_weight(0, IM)
        for c in range(1, C):
            load_weight(c, RE)
            load_weight(c, IM)
            if c % 2 == 0:
                load_scales(nc.sync, c // 2)
            load_g(c)

        split = {}
        grouped = {}
        codes = {}
        scales = {}
        real = {}
        minuend = {}
        diff = {}
        results = {}

        def split_pairs(copy, c, part, passes, rows=slice(0, ROWS)):
            if (c, part) not in split:
                split[c, part] = work.tile([P, ROWS, PASSES, 2, P], F32, name="split", bufs=2)
            pairs = raw[c, part][:].bitcast(F32).rearrange("p (q g k u) -> p q g u k", q=ROWS, g=PASSES, u=2)
            copy(out=split[c, part][:, rows, passes], in_=pairs[:, rows, passes])

        def transposes(c, part):
            for g in range(PASSES):
                grouped[c, part, g] = work.tile([P, 4 * I], BF16, name="grouped", align_bytes=64)
            if (c, part) == (0, RE):
                order = [(g, j) for j in range(2) for g in range(PASSES)]
            else:
                order = [(g, j) for g in range(PASSES) for j in range(2)]
            for g, j in order:
                bank = tpsum.tile([P, 4, P], F32, name="bank")
                for slot in range(4):
                    nc.tensor.transpose(bank[:, slot, :], split[c, part][:, 2 * j + slot // 2, g, slot % 2, :], ident[:])
                nc.scalar.copy(
                    out=grouped[c, part, g][:].bitcast(F32).rearrange("k (p j slot) -> k j p slot", j=2, slot=4)[:, j],
                    in_=bank[:].rearrange("k slot p -> k p slot"),
                )

        def quantise(c, part, g):
            codes[c, part, g] = qpool.tile([P, I], U32, name="codes", align_bytes=64)
            scales[c, part, g] = qpool.tile([P, I], U8, name="scales", align_bytes=64)
            nc.vector.quantize_mx(out=codes[c, part, g][:].bitcast(E4M3), scales=scales[c, part, g][:], in_=grouped[c, part, g][:])

        def one_pass(acc, c, dy_part, t, w_part, g, start, stop):
            col = B * dy_part + P * t
            plane_col = G_COLS * (c % 2) + col
            nc.tensor.matmul_mx(
                out=acc[:],
                lhsT=g_codes[:, c, g, col : col + P].bitcast(E5M2),
                lhsT_scale=g_planes[:, c // 2, g, plane_col : plane_col + P],
                rhs=codes[c, w_part, g][:].bitcast(E4M3),
                rhs_scale=scales[c, w_part, g][:],
                start=start,
                stop=stop,
            )

        def products_with_w_re(c):
            cross = [apsum.tile([P, I], F32, name="cross") for t in range(TILES)]
            for g in range(PASSES):
                for t in range(TILES):
                    one_pass(cross[t], c, IM, t, RE, g, g == 0, g == PASSES - 1)
            for t in range(TILES):
                minuend[t] = work.tile([P, I], F32, name="minuend", bufs=TILES)
                nc.scalar.copy(out=minuend[t][:], in_=cross[t][:])
            for t in range(TILES):
                real[t] = apsum.tile([P, I], F32, name="real")
                for g in range(PASSES):
                    one_pass(real[t], c, RE, t, RE, g, g == 0, False)

        def products_with_w_im(c):
            cross = [apsum.tile([P, I], F32, name="cross") for t in range(TILES)]
            for t in range(TILES):
                for g in range(PASSES):
                    one_pass(cross[t], c, RE, t, IM, g, g == 0, g == PASSES - 1)
                for g in range(PASSES):
                    one_pass(real[t], c, IM, t, IM, g, False, g == PASSES - 1)
            return cross

        def subtract(t, subtrahend):
            diff[t] = work.tile([P, I], F32, name="diff", bufs=TILES)
            nc.vector.tensor_tensor(out=diff[t][:], in0=minuend[t][:], in1=subtrahend[:], op=SUB)

        def apply_gain(engine, c, part, t):
            if (c, part) not in results:
                results[c, part] = keep.tile([P, TILES, I], F32, name="result_%d_%d" % (c, part))
            engine.tensor_tensor(out=results[c, part][:, t], in0=(real, diff)[part][t][:], in1=gain_all[:, I * c : I * (c + 1)], op=MULT)

        both_passes = slice(0, PASSES)
        first_pass, second_pass = slice(0, 1), slice(1, 2)

        gain_wide = keep.tile([P, 4 * GROUPS, P], F32, name="gain_wide")
        gain_pairs = gain_rows[:].rearrange("p s j -> p (s j)").bitcast(F32)
        for j in range(2):
            for passes in (first_pass, second_pass):
                split_pairs(nc.vector.tensor_copy, 0, RE, passes, slice(2 * j, 2 * j + 2))
        nc.vector.tensor_copy(out=gain_wide[:], in_=gain_pairs.unsqueeze(2).to_broadcast([P, 4 * GROUPS, P]))
        transposes(0, RE)

        gain_all = keep.tile([P, C * I], BF16, name="gain_all")
        for group in range(GROUPS):
            bank = tpsum.tile([P, 4, P], F32, name="bank")
            for slot in range(4):
                nc.tensor.transpose(bank[:, slot, :], gain_wide[:, 4 * group + slot, :], ident[:])
            nc.scalar.copy(
                out=gain_all[:].bitcast(F32)[:, I * group : I * (group + 1)].rearrange("m (p slot) -> m p slot", slot=4),
                in_=bank[:].rearrange("m slot p -> m p slot"),
            )

        quantise(0, RE, 0)
        quantise(0, RE, 1)
        products_with_w_re(0)
        split_pairs(nc.vector.tensor_copy, 0, IM, first_pass)
        split_pairs(nc.vector.tensor_copy, 0, IM, second_pass)
        transposes(0, IM)
        split_pairs(nc.vector.tensor_copy, 1, RE, first_pass)
        split_pairs(nc.vector.tensor_copy, 1, RE, second_pass)
        quantise(0, IM, 0)
        quantise(0, IM, 1)
        transposes(1, RE)
        split_pairs(nc.vector.tensor_copy, 1, IM, first_pass)

        for c in range(C):
            has_next = c + 1 < C
            has_second_next = c + 2 < C
            if 0 < c <= EARLY_STORES:
                for part in (RE, IM):
                    nc.gpsimd.dma_start(out=outs[part][c - 1].rearrange("(t p) i -> p t i", p=P), in_=results[c - 1, part][:])
            if has_next:
                split_pairs(nc.scalar.copy, c + 1, IM, second_pass)
                quantise(c + 1, RE, 0)
            subtrahend = products_with_w_im(c)
            subtract(0, subtrahend[0])
            apply_gain(nc.gpsimd, c, IM, 0)
            apply_gain(nc.vector, c, RE, 0)
            subtract(1, subtrahend[1])
            apply_gain(nc.vector, c, RE, 1)
            if has_next:
                quantise(c + 1, RE, 1)
                transposes(c + 1, IM)
                products_with_w_re(c + 1)
            if has_second_next:
                split_pairs(nc.vector.tensor_copy, c + 2, RE, both_passes)
            if has_next:
                quantise(c + 1, IM, 0)
                quantise(c + 1, IM, 1)
            if has_second_next:
                transposes(c + 2, RE)
                split_pairs(nc.vector.tensor_copy, c + 2, IM, first_pass)
            apply_gain(nc.vector, c, IM, 1)

        for c in range(EARLY_STORES, C):
            for t in range(TILES):
                for part in (RE, IM):
                    nc.sync.dma_start(out=outs[part][c, P * t : P * (t + 1), :], in_=results[c, part][:, t])
